import numpy as np
import ml_dtypes


def mxq(x, axis, fmt="e4m3"):
    dtype, down = {"e4m3": (ml_dtypes.float8_e4m3fn, 7), "e5m2": (ml_dtypes.float8_e5m2, 14)}[fmt]
    v = np.moveaxis(np.asarray(x, np.float32).astype(ml_dtypes.bfloat16).astype(np.float64), axis, -1)
    blocks = v.reshape(v.shape[:-1] + (-1, 32))
    amax = np.abs(blocks).max(-1, keepdims=True)
    byte = np.maximum(np.where(amax > 0, np.frexp(amax)[1] - 1 + 127, 0) - down, 1)
    scale = np.exp2(byte - 127.0)
    codes = (blocks / scale).astype(np.float32).astype(dtype).astype(np.float64)
    return np.moveaxis((codes * scale).reshape(v.shape), -1, axis)


WIDE = False


def mx_kscale(k):
    if not WIDE:
        return np.ones(k)
    levels = np.array([10, -10, 5, -5, 0])
    if k % 512:
        return np.exp2(np.random.permutation(np.resize(levels, k // 32))).repeat(32)
    a = np.empty((k // 512, 16))
    for p in range(k // 512):
        a[p, :8] = np.random.permutation(np.resize(levels, 8))
        for g in range(8):
            far = levels[np.abs(levels - a[p, g]) >= 10]
            a[p, g + 8] = far[np.random.randint(len(far))]
    return np.exp2(a.ravel()).repeat(32)


def f64(x):
    return np.asarray(x).astype(np.float64)


def striped(idx):
    return np.tile(idx.reshape(-1, 16).T, (8, 1)).astype(np.uint16)


def unstriped(offs):
    return offs[:16].T.reshape(-1).astype(np.int64)


def pack_weight(w):
    k, n = w.shape
    w = f64(np.asarray(w, np.float32).astype(ml_dtypes.bfloat16)).reshape(k // 32, 32, n)
    amax = np.abs(w).max(1)
    byte = np.clip(np.where(amax > 0, np.frexp(amax)[1] - 1 + 127 - 7, 1), 1, 254)
    scaled = (w * np.exp2(127.0 - byte)[:, None, :]).reshape(k, n).astype(np.float32)
    words = np.ascontiguousarray(scaled.reshape(k // 512, 128, 4, n).transpose(0, 1, 3, 2)).astype(ml_dtypes.float8_e4m3fn).view(np.uint8)
    return words, np.ascontiguousarray(byte.astype(np.uint8).reshape(k // 512, 16, n))


def unpack_weight(words, scales):
    g, p, n, _ = words.shape
    vals = np.ascontiguousarray(words).view(ml_dtypes.float8_e4m3fn).astype(np.float64) * np.repeat(np.exp2(scales.astype(np.float64) - 127.0), 8, axis=1)[..., None]
    return vals.transpose(0, 1, 3, 2).reshape(g * 512, n)


K, T, E, C, N = 1024, 1024, 4, 128, 512


def by_expert(wq, xq):
    return np.concatenate([wq[e].T @ xq[:, e * C:(e + 1) * C] for e in range(E)], axis=1)


def setup_inputs():
    n = np.random.standard_normal
    s = mx_kscale(K)[:, None]
    packed = [pack_weight(m) for m in n((E, K, N)) / np.sqrt(K) / s[None]]
    return {
        "xT": (n((K, T)) * s).astype(np.float32),
        "w_words": np.stack([m[0] for m in packed]),
        "w_scales": np.stack([m[1] for m in packed]),
        "gate": np.tile(np.random.uniform(0.2, 1.0, E * C), (N, 1)).astype(np.float32),
        "offs": striped(np.random.permutation(T)[:E * C]),
    }


def reference(xT, w_words, w_scales, gate, offs):
    idx = unstriped(offs)
    xq = mxq(f64(xT)[:, idx], 0, "e4m3")
    w = np.stack([unpack_weight(w_words[e], w_scales[e]) for e in range(E)])
    y = by_expert(w, xq)
    out = np.zeros((N, T))
    out[:, idx] = f64(gate) * y
    return out

@@ -1,0 +1,126 @@
+from contextlib import ExitStack
+
+import concourse.mybir as mybir
+
+K, T, E, C, N = 1024, 1024, 4, 128, 512
+FLOPS = 2 * K * N * E * C
+
+F32 = mybir.dt.float32
+BF16 = mybir.dt.bfloat16
+I32 = mybir.dt.int32
+U32 = mybir.dt.uint32
+U16 = mybir.dt.uint16
+U8 = mybir.dt.uint8
+FP8X4 = mybir.dt.float8_e4m3fn_x4
+MULT = mybir.AluOpType.mult
+
+P = 128
+PACK = 4
+K_PASS = P * PACK
+PASSES = K // K_PASS
+SLOTS = E * C
+BLOCKS = N // P
+CUT = 256
+CUTS = SLOTS // CUT
+CUT_EXPERTS = CUT // C
+CUT_COLS = CUT // 16
+
+
+def tile_routed_moe_kernel(tc, xT, w_words, w_scales, gate, offs, out):
+    nc = tc.nc
+    with ExitStack() as ctx:
+        lists = ctx.enter_context(tc.tile_pool(name="lists", bufs=1))
+        keep = ctx.enter_context(tc.tile_pool(name="keep", bufs=1))
+        psum = ctx.enter_context(tc.psum_pool(name="psum", bufs=1))
+
+        offsets = lists.tile([P, SLOTS // 16], U16, name="offsets")
+        nc.sync.dma_start(offsets[:], offs)
+
+        planes_hbm = xT.rearrange("(g p t) n -> g p t n", p=P, t=PACK)
+        x_plane = {}
+        for g in range(PASSES):
+            for t in range(PACK):
+                x_plane[g, t] = keep.tile([P, T], F32, name="x_plane_%d_%d" % (g, t))
+                nc.sync.dma_start(x_plane[g, t][:], planes_hbm[g, :, t, :])
+
+        w_plane = keep.tile([P, E * PASSES, N], U8, name="w_plane", align_bytes=64)
+        nc.vector.memset(w_plane[:].rearrange("p j n -> p (j n)").bitcast(I32), 0)
+        scales_hbm = w_scales.rearrange("e a (q r) n -> r q (e a) n", r=4)
+        for r in range(4):
+            nc.sync.dma_start(w_plane[r:P:32, :, :].bitcast(I32), scales_hbm[r].bitcast(I32))
+
+        w_codes = {}
+        gate_sb = {}
+
+        def load_weights(e):
+            w_codes[e] = keep.tile([P, PASSES, N], I32, name="w_codes_%d" % e, align_bytes=64)
+            nc.sync.dma_start(w_codes[e][:], w_words[e].rearrange("a p n r -> p a (n r)").bitcast(I32))
+
+        def load_gate(b):
+            gate_sb[b] = keep.tile([P, SLOTS], F32, name="gate_sb_%d" % b)
+            nc.sync.dma_start(gate_sb[b][:], gate[b * P:(b + 1) * P, :])
+
+        load_weights(0)
+        load_weights(1)
+        load_gate(0)
+        load_weights(2)
+        load_weights(3)
+        for b in range(1, BLOCKS):
+            load_gate(b)
+
+        window = {}
+        for b in range(BLOCKS):
+            window[b] = keep.tile([P, T], F32, name="window_%d" % b)
+            nc.vector.memset(window[b][:], 0.0)
+
+        warm_in = keep.tile([P, 8], F32, name="warm_in")
+        warm_out = keep.tile([P, 8], F32, name="warm_out")
+        nc.vector.memset(warm_in[:], 0.0)
+        nc.scalar.copy(out=warm_out[:], in_=warm_in[:])
+
+        x_codes = {}
+        x_scales = {}
+        for g in range(PASSES):
+            for h in range(CUTS):
+                cols = offsets[:, h * CUT_COLS:(h + 1) * CUT_COLS]
+                picked = keep.tile([P, PACK, CUT], F32, name="picked_%d_%d" % (g, h))
+                for t in range(PACK):
+                    nc.vector.tensor_copy(out=picked[:, t, :], in_=x_plane[g, t][:].indirect(cols))
+                grouped = keep.tile([P, CUT, PACK], BF16, name="grouped_%d_%d" % (g, h), align_bytes=64)
+                nc.scalar.copy(out=grouped[:], in_=picked[:].rearrange("p t c -> p c t"))
+                x_codes[g, h] = keep.tile([P, CUT], U32, name="x_codes_%d_%d" % (g, h), align_bytes=64)
+                x_scales[g, h] = keep.tile([P, CUT], U8, name="x_scales_%d_%d" % (g, h), align_bytes=64)
+                nc.vector.quantize_mx(
+                    out=x_codes[g, h][:].bitcast(FP8X4),
+                    scales=x_scales[g, h][:],
+                    in_=grouped[:].rearrange("p c t -> p (c t)"),
+                )
+
+        for h in range(CUTS):
+            cols = offsets[:, h * CUT_COLS:(h + 1) * CUT_COLS]
+            for b in range(BLOCKS):
+                feats = slice(b * P, (b + 1) * P)
+                acc = psum.tile([P, CUT], F32, name="acc_%d_%d" % (b, h))
+                for i in range(CUT_EXPERTS):
+                    e = h * CUT_EXPERTS + i
+                    places = slice(i * C, (i + 1) * C)
+                    for g in range(PASSES):
+                        nc.tensor.matmul_mx(
+                            out=acc[:, places],
+                            lhsT=w_codes[e][:, g, feats].bitcast(FP8X4),
+                            lhsT_scale=w_plane[:, e * PASSES + g, feats],
+                            rhs=x_codes[g, h][:, places].bitcast(FP8X4),
+                            rhs_scale=x_scales[g, h][:, places],
+                            start=(g == 0),
+                            stop=(g == PASSES - 1),
+                        )
+                sums = keep.tile([P, CUT], F32, name="sums_%d_%d" % (b, h))
+                nc.scalar.copy(out=sums[:], in_=acc[:])
+                nc.vector.tensor_tensor(
+                    out=window[b][:].indirect(cols),
+                    in0=sums[:],
+                    in1=gate_sb[b][:, h * CUT:(h + 1) * CUT],
+                    op=MULT,
+                )
+                if h == CUTS - 1:
+                    nc.sync.dma_start(out[feats, :], window[b][:])

@@ -38,19 +38,19 @@ def tile_routed_moe_kernel(tc, xT, w_words, w_scales, gate, offs, out):
 
         planes_hbm = xT.rearrange("(g p t) n -> g p t n", p=P, t=PACK)
         x_plane = {}
-        for g in range(PASSES):
-            for t in range(PACK):
-                x_plane[g, t] = keep.tile([P, T], F32, name="x_plane_%d_%d" % (g, t))
-                nc.sync.dma_start(x_plane[g, t][:], planes_hbm[g, :, t, :])
-
-        w_plane = keep.tile([P, E * PASSES, N], U8, name="w_plane", align_bytes=64)
-        nc.vector.memset(w_plane[:].rearrange("p j n -> p (j n)").bitcast(I32), 0)
-        scales_hbm = w_scales.rearrange("e a (q r) n -> r q (e a) n", r=4)
-        for r in range(4):
-            nc.sync.dma_start(w_plane[r:P:32, :, :].bitcast(I32), scales_hbm[r].bitcast(I32))
-
         w_codes = {}
         gate_sb = {}
+        window = {}
+        picked = {}
+        grouped = {}
+        x_codes = {}
+        x_scales = {}
+        acc = {}
+        sums = {}
+
+        def load_plane(g, t):
+            x_plane[g, t] = keep.tile([P, T], F32, name="x_plane_%d_%d" % (g, t))
+            nc.sync.dma_start(x_plane[g, t][:], planes_hbm[g, :, t, :])
 
         def load_weights(e):
             w_codes[e] = keep.tile([P, PASSES, N], I32, name="w_codes_%d" % e, align_bytes=64)
@@ -60,6 +60,18 @@ def tile_routed_moe_kernel(tc, xT, w_words, w_scales, gate, offs, out):
             gate_sb[b] = keep.tile([P, SLOTS], F32, name="gate_sb_%d" % b)
             nc.sync.dma_start(gate_sb[b][:], gate[b * P:(b + 1) * P, :])
 
+        w_plane = keep.tile([P, E * PASSES, N], U8, name="w_plane", align_bytes=64)
+        nc.gpsimd.memset(w_plane[:].rearrange("p j n -> p (j n)").bitcast(F32), 0.0)
+        scales_hbm = w_scales.rearrange("e a (q r) n -> r q (e a) n", r=4)
+
+        for t in range(PACK):
+            load_plane(0, t)
+        load_plane(1, 0)
+        load_plane(1, 1)
+        for r in range(4):
+            nc.sync.dma_start(w_plane[r:P:32, :, :].bitcast(I32), scales_hbm[r].bitcast(I32))
+        load_plane(1, 2)
+        load_plane(1, 3)
         load_weights(0)
         load_weights(1)
         load_gate(0)
@@ -68,59 +80,81 @@ def tile_routed_moe_kernel(tc, xT, w_words, w_scales, gate, offs, out):
         for b in range(1, BLOCKS):
             load_gate(b)
 
-        window = {}
         for b in range(BLOCKS):
             window[b] = keep.tile([P, T], F32, name="window_%d" % b)
-            nc.vector.memset(window[b][:], 0.0)
+            if b < 2:
+                nc.vector.memset(window[b][:], 0.0)
+            else:
+                nc.gpsimd.memset(window[b][:], 0.0)
 
         warm_in = keep.tile([P, 8], F32, name="warm_in")
         warm_out = keep.tile([P, 8], F32, name="warm_out")
-        nc.vector.memset(warm_in[:], 0.0)
+        nc.gpsimd.memset(warm_in[:], 0.0)
         nc.scalar.copy(out=warm_out[:], in_=warm_in[:])
 
-        x_codes = {}
-        x_scales = {}
-        for g in range(PASSES):
-            for h in range(CUTS):
-                cols = offsets[:, h * CUT_COLS:(h + 1) * CUT_COLS]
-                picked = keep.tile([P, PACK, CUT], F32, name="picked_%d_%d" % (g, h))
-                for t in range(PACK):
-                    nc.vector.tensor_copy(out=picked[:, t, :], in_=x_plane[g, t][:].indirect(cols))
-                grouped = keep.tile([P, CUT, PACK], BF16, name="grouped_%d_%d" % (g, h), align_bytes=64)
-                nc.scalar.copy(out=grouped[:], in_=picked[:].rearrange("p t c -> p c t"))
-                x_codes[g, h] = keep.tile([P, CUT], U32, name="x_codes_%d_%d" % (g, h), align_bytes=64)
-                x_scales[g, h] = keep.tile([P, CUT], U8, name="x_scales_%d_%d" % (g, h), align_bytes=64)
-                nc.vector.quantize_mx(
-                    out=x_codes[g, h][:].bitcast(FP8X4),
-                    scales=x_scales[g, h][:],
-                    in_=grouped[:].rearrange("p c t -> p (c t)"),
-                )
+        def cols(h):
+            return offsets[:, h * CUT_COLS:(h + 1) * CUT_COLS]
+
+        def gather(g, h, t):
+            if t == 0:
+                picked[g, h] = keep.tile([P, PACK, CUT], F32, name="picked_%d_%d" % (g, h))
+            nc.vector.tensor_copy(out=picked[g, h][:, t, :], in_=x_plane[g, t][:].indirect(cols(h)))
+
+        def interleave(g, h):
+            grouped[g, h] = keep.tile([P, CUT, PACK], BF16, name="grouped_%d_%d" % (g, h), align_bytes=64)
+            nc.scalar.copy(out=grouped[g, h][:], in_=picked[g, h][:].rearrange("p t c -> p c t"))
+
+        def quantize(g, h):
+            x_codes[g, h] = keep.tile([P, CUT], U32, name="x_codes_%d_%d" % (g, h), align_bytes=64)
+            x_scales[g, h] = keep.tile([P, CUT], U8, name="x_scales_%d_%d" % (g, h), align_bytes=64)
+            nc.vector.quantize_mx(
+                out=x_codes[g, h][:].bitcast(FP8X4),
+                scales=x_scales[g, h][:],
+                in_=grouped[g, h][:].rearrange("p c t -> p (c t)"),
+            )
+
+        def multiply(b, h):
+            feats = slice(b * P, (b + 1) * P)
+            acc[b, h] = psum.tile([P, CUT], F32, name="acc_%d_%d" % (b, h))
+            for i in range(CUT_EXPERTS):
+                e = h * CUT_EXPERTS + i
+                places = slice(i * C, (i + 1) * C)
+                for g in range(PASSES):
+                    nc.tensor.matmul_mx(
+                        out=acc[b, h][:, places],
+                        lhsT=w_codes[e][:, g, feats].bitcast(FP8X4),
+                        lhsT_scale=w_plane[:, e * PASSES + g, feats],
+                        rhs=x_codes[g, h][:, places].bitcast(FP8X4),
+                        rhs_scale=x_scales[g, h][:, places],
+                        start=(g == 0),
+                        stop=(g == PASSES - 1),
+                    )
+
+        def copy_out(b, h):
+            sums[b, h] = keep.tile([P, CUT], F32, name="sums_%d_%d" % (b, h))
+            nc.scalar.copy(out=sums[b, h][:], in_=acc[b, h][:])
+
+        def scatter(b, h):
+            nc.vector.tensor_tensor(
+                out=window[b][:].indirect(cols(h)),
+                in0=sums[b, h][:],
+                in1=gate_sb[b][:, h * CUT:(h + 1) * CUT],
+                op=MULT,
+            )
+
+        def store(b):
+            nc.sync.dma_start(out[b * P:(b + 1) * P, :], window[b][:])
 
         for h in range(CUTS):
-            cols = offsets[:, h * CUT_COLS:(h + 1) * CUT_COLS]
+            for g in range(PASSES):
+                for t in range(PACK):
+                    gather(g, h, t)
+                interleave(g, h)
+                quantize(g, h)
+        for h in range(CUTS):
             for b in range(BLOCKS):
-                feats = slice(b * P, (b + 1) * P)
-                acc = psum.tile([P, CUT], F32, name="acc_%d_%d" % (b, h))
-                for i in range(CUT_EXPERTS):
-                    e = h * CUT_EXPERTS + i
-                    places = slice(i * C, (i + 1) * C)
-                    for g in range(PASSES):
-                        nc.tensor.matmul_mx(
-                            out=acc[:, places],
-                            lhsT=w_codes[e][:, g, feats].bitcast(FP8X4),
-                            lhsT_scale=w_plane[:, e * PASSES + g, feats],
-                            rhs=x_codes[g, h][:, places].bitcast(FP8X4),
-                            rhs_scale=x_scales[g, h][:, places],
-                            start=(g == 0),
-                            stop=(g == PASSES - 1),
-                        )
-                sums = keep.tile([P, CUT], F32, name="sums_%d_%d" % (b, h))
-                nc.scalar.copy(out=sums[:], in_=acc[:])
-                nc.vector.tensor_tensor(
-                    out=window[b][:].indirect(cols),
-                    in0=sums[:],
-                    in1=gate_sb[b][:, h * CUT:(h + 1) * CUT],
-                    op=MULT,
-                )
+                multiply(b, h)
+                copy_out(b, h)
+                scatter(b, h)
                 if h == CUTS - 1:
-                    nc.sync.dma_start(out[feats, :], window[b][:])
+                    store(b)

@@ -20,10 +20,9 @@ K_PASS = P * PACK
 PASSES = K // K_PASS
 SLOTS = E * C
 BLOCKS = N // P
-CUT = 256
-CUTS = SLOTS // CUT
-CUT_EXPERTS = CUT // C
-CUT_COLS = CUT // 16
+
+CUTS = ((0, 128), (128, 512))
+PAD = 16
 
 
 def tile_routed_moe_kernel(tc, xT, w_words, w_scales, gate, offs, out):
@@ -36,125 +35,97 @@ def tile_routed_moe_kernel(tc, xT, w_words, w_scales, gate, offs, out):
         offsets = lists.tile([P, SLOTS // 16], U16, name="offsets")
         nc.sync.dma_start(offsets[:], offs)
 
+        def listed(lo, hi):
+            return offsets[:, lo // 16:hi // 16]
+
         planes_hbm = xT.rearrange("(g p t) n -> g p t n", p=P, t=PACK)
-        x_plane = {}
+        plane = {}
+        for g in range(PASSES):
+            for t in range(PACK):
+                plane[g, t] = keep.tile([P, T + PAD], F32, name="plane_%d_%d" % (g, t))
+                nc.sync.dma_start(plane[g, t][:, 0:T], planes_hbm[g, :, t, :])
+
+        w_plane = keep.tile([P, E * PASSES, N], U8, name="w_plane", align_bytes=64)
+        nc.vector.memset(w_plane[:].rearrange("p j n -> p (j n)").bitcast(I32), 0)
+        scales_hbm = w_scales.rearrange("e a (q r) n -> r q (e a) n", r=4)
+        for r in range(4):
+            nc.sync.dma_start(w_plane[r:P:32, :, :].bitcast(I32), scales_hbm[r].bitcast(I32))
+
         w_codes = {}
         gate_sb = {}
-        window = {}
-        picked = {}
-        grouped = {}
-        x_codes = {}
-        x_scales = {}
-        acc = {}
-        sums = {}
-
-        def load_plane(g, t):
-            x_plane[g, t] = keep.tile([P, T], F32, name="x_plane_%d_%d" % (g, t))
-            nc.sync.dma_start(x_plane[g, t][:], planes_hbm[g, :, t, :])
+        gate_hbm = gate.rearrange("(b p) j -> p b j", p=P)
 
         def load_weights(e):
             w_codes[e] = keep.tile([P, PASSES, N], I32, name="w_codes_%d" % e, align_bytes=64)
             nc.sync.dma_start(w_codes[e][:], w_words[e].rearrange("a p n r -> p a (n r)").bitcast(I32))
 
-        def load_gate(b):
-            gate_sb[b] = keep.tile([P, SLOTS], F32, name="gate_sb_%d" % b)
-            nc.sync.dma_start(gate_sb[b][:], gate[b * P:(b + 1) * P, :])
+        def load_gate(lo, hi):
+            gate_sb[lo] = keep.tile([P, BLOCKS, hi - lo], F32, name="gate_sb_%d" % lo)
+            nc.sync.dma_start(gate_sb[lo][:], gate_hbm[:, :, lo:hi])
 
-        w_plane = keep.tile([P, E * PASSES, N], U8, name="w_plane", align_bytes=64)
-        nc.gpsimd.memset(w_plane[:].rearrange("p j n -> p (j n)").bitcast(F32), 0.0)
-        scales_hbm = w_scales.rearrange("e a (q r) n -> r q (e a) n", r=4)
-
-        for t in range(PACK):
-            load_plane(0, t)
-        load_plane(1, 0)
-        load_plane(1, 1)
-        for r in range(4):
-            nc.sync.dma_start(w_plane[r:P:32, :, :].bitcast(I32), scales_hbm[r].bitcast(I32))
-        load_plane(1, 2)
-        load_plane(1, 3)
         load_weights(0)
+        load_gate(0, 128)
         load_weights(1)
-        load_gate(0)
         load_weights(2)
         load_weights(3)
-        for b in range(1, BLOCKS):
-            load_gate(b)
+        load_gate(128, 512)
 
+        window = {}
         for b in range(BLOCKS):
             window[b] = keep.tile([P, T], F32, name="window_%d" % b)
-            if b < 2:
-                nc.vector.memset(window[b][:], 0.0)
-            else:
-                nc.gpsimd.memset(window[b][:], 0.0)
+            nc.vector.memset(window[b][:], 0.0)
 
         warm_in = keep.tile([P, 8], F32, name="warm_in")
         warm_out = keep.tile([P, 8], F32, name="warm_out")
-        nc.gpsimd.memset(warm_in[:], 0.0)
+        nc.vector.memset(warm_in[:], 0.0)
         nc.scalar.copy(out=warm_out[:], in_=warm_in[:])
 
-        def cols(h):
-            return offsets[:, h * CUT_COLS:(h + 1) * CUT_COLS]
+        grouped = {}
+        x_codes = {}
+        x_scales = {}
+        for g in range(PASSES):
+            grouped[g] = keep.tile([P, SLOTS, PACK], BF16, name="grouped_%d" % g, align_bytes=64)
+            x_codes[g] = keep.tile([P, SLOTS], U32, name="x_codes_%d" % g, align_bytes=64)
+            x_scales[g] = keep.tile([P, SLOTS], U8, name="x_scales_%d" % g, align_bytes=64)
 
-        def gather(g, h, t):
-            if t == 0:
-                picked[g, h] = keep.tile([P, PACK, CUT], F32, name="picked_%d_%d" % (g, h))
-            nc.vector.tensor_copy(out=picked[g, h][:, t, :], in_=x_plane[g, t][:].indirect(cols(h)))
-
-        def interleave(g, h):
-            grouped[g, h] = keep.tile([P, CUT, PACK], BF16, name="grouped_%d_%d" % (g, h), align_bytes=64)
-            nc.scalar.copy(out=grouped[g, h][:], in_=picked[g, h][:].rearrange("p t c -> p c t"))
-
-        def quantize(g, h):
-            x_codes[g, h] = keep.tile([P, CUT], U32, name="x_codes_%d_%d" % (g, h), align_bytes=64)
-            x_scales[g, h] = keep.tile([P, CUT], U8, name="x_scales_%d_%d" % (g, h), align_bytes=64)
+        def quantize(g, lo, hi):
             nc.vector.quantize_mx(
-                out=x_codes[g, h][:].bitcast(FP8X4),
-                scales=x_scales[g, h][:],
-                in_=grouped[g, h][:].rearrange("p c t -> p (c t)"),
+                out=x_codes[g][:, lo:hi].bitcast(FP8X4),
+                scales=x_scales[g][:, lo:hi],
+                in_=grouped[g][:, lo:hi, :].rearrange("p c t -> p (c t)"),
             )
 
-        def multiply(b, h):
-            feats = slice(b * P, (b + 1) * P)
-            acc[b, h] = psum.tile([P, CUT], F32, name="acc_%d_%d" % (b, h))
-            for i in range(CUT_EXPERTS):
-                e = h * CUT_EXPERTS + i
-                places = slice(i * C, (i + 1) * C)
-                for g in range(PASSES):
-                    nc.tensor.matmul_mx(
-                        out=acc[b, h][:, places],
-                        lhsT=w_codes[e][:, g, feats].bitcast(FP8X4),
-                        lhsT_scale=w_plane[:, e * PASSES + g, feats],
-                        rhs=x_codes[g, h][:, places].bitcast(FP8X4),
-                        rhs_scale=x_scales[g, h][:, places],
-                        start=(g == 0),
-                        stop=(g == PASSES - 1),
-                    )
+        for g in range(PASSES):
+            for t in range(PACK):
+                for lo, hi in CUTS:
+                    nc.vector.tensor_copy(out=grouped[g][:, lo:hi, t], in_=plane[g, t][:, 0:T].indirect(listed(lo, hi)))
+        quantize(0, 0, 512)
+        quantize(1, 0, 128)
+        quantize(1, 128, 256)
+        quantize(1, 256, 512)
 
-        def copy_out(b, h):
-            sums[b, h] = keep.tile([P, CUT], F32, name="sums_%d_%d" % (b, h))
-            nc.scalar.copy(out=sums[b, h][:], in_=acc[b, h][:])
-
-        def scatter(b, h):
-            nc.vector.tensor_tensor(
-                out=window[b][:].indirect(cols(h)),
-                in0=sums[b, h][:],
-                in1=gate_sb[b][:, h * CUT:(h + 1) * CUT],
-                op=MULT,
-            )
-
-        def store(b):
-            nc.sync.dma_start(out[b * P:(b + 1) * P, :], window[b][:])
-
-        for h in range(CUTS):
-            for g in range(PASSES):
-                for t in range(PACK):
-                    gather(g, h, t)
-                interleave(g, h)
-                quantize(g, h)
-        for h in range(CUTS):
+        for lo, hi in CUTS:
             for b in range(BLOCKS):
-                multiply(b, h)
-                copy_out(b, h)
-                scatter(b, h)
-                if h == CUTS - 1:
-                    store(b)
+                feats = slice(b * P, (b + 1) * P)
+                acc = psum.tile([P, hi - lo], F32, name="acc_%d_%d" % (b, lo))
+                for e in range(lo // C, hi // C):
+                    for g in range(PASSES):
+                        nc.tensor.matmul_mx(
+                            out=acc[:, e * C - lo:(e + 1) * C - lo],
+                            lhsT=w_codes[e][:, g, feats].bitcast(FP8X4),
+                            lhsT_scale=w_plane[:, e * PASSES + g, feats],
+                            rhs=x_codes[g][:, e * C:(e + 1) * C].bitcast(FP8X4),
+                            rhs_scale=x_scales[g][:, e * C:(e + 1) * C],
+                            start=(g == 0),
+                            stop=(g == PASSES - 1),
+                        )
+                sums = keep.tile([P, hi - lo], F32, name="sums_%d_%d" % (b, lo))
+                nc.scalar.copy(out=sums[:], in_=acc[:])
+                nc.vector.tensor_tensor(
+                    out=window[b][:].indirect(listed(lo, hi)),
+                    in0=sums[:],
+                    in1=gate_sb[lo][:, b, :],
+                    op=MULT,
+                )
+                if hi == SLOTS:
+                    nc.sync.dma_start(out[feats, :], window[b][:])

@@ -23,6 +23,7 @@ BLOCKS = N // P
 
 CUTS = ((0, 128), (128, 512))
 PAD = 16
+DIRECT = (1, 1)
 
 
 def tile_routed_moe_kernel(tc, xT, w_words, w_scales, gate, offs, out):
@@ -42,11 +43,12 @@ def tile_routed_moe_kernel(tc, xT, w_words, w_scales, gate, offs, out):
         plane = {}
         for g in range(PASSES):
             for t in range(PACK):
-                plane[g, t] = keep.tile([P, T + PAD], F32, name="plane_%d_%d" % (g, t))
+                width = T + PAD if (g, t // 2) == DIRECT else T
+                plane[g, t] = keep.tile([P, width], F32, name="plane_%d_%d" % (g, t))
                 nc.sync.dma_start(plane[g, t][:, 0:T], planes_hbm[g, :, t, :])
 
         w_plane = keep.tile([P, E * PASSES, N], U8, name="w_plane", align_bytes=64)
-        nc.vector.memset(w_plane[:].rearrange("p j n -> p (j n)").bitcast(I32), 0)
+        nc.gpsimd.memset(w_plane[:].rearrange("p j n -> p (j n)").bitcast(F32), 0.0)
         scales_hbm = w_scales.rearrange("e a (q r) n -> r q (e a) n", r=4)
         for r in range(4):
             nc.sync.dma_start(w_plane[r:P:32, :, :].bitcast(I32), scales_hbm[r].bitcast(I32))
@@ -59,25 +61,27 @@ def tile_routed_moe_kernel(tc, xT, w_words, w_scales, gate, offs, out):
             w_codes[e] = keep.tile([P, PASSES, N], I32, name="w_codes_%d" % e, align_bytes=64)
             nc.sync.dma_start(w_codes[e][:], w_words[e].rearrange("a p n r -> p a (n r)").bitcast(I32))
 
-        def load_gate(lo, hi):
-            gate_sb[lo] = keep.tile([P, BLOCKS, hi - lo], F32, name="gate_sb_%d" % lo)
-            nc.sync.dma_start(gate_sb[lo][:], gate_hbm[:, :, lo:hi])
-
         load_weights(0)
-        load_gate(0, 128)
+        gate_first = keep.tile([P, BLOCKS, C], F32, name="gate_first")
+        nc.sync.dma_start(gate_first[:], gate_hbm[:, :, 0:C])
         load_weights(1)
         load_weights(2)
         load_weights(3)
-        load_gate(128, 512)
+        for b in range(BLOCKS):
+            gate_sb[b] = keep.tile([P, SLOTS - C], F32, name="gate_sb_%d" % b)
+            nc.sync.dma_start(gate_sb[b][:], gate[b * P:(b + 1) * P, C:SLOTS])
 
         window = {}
         for b in range(BLOCKS):
             window[b] = keep.tile([P, T], F32, name="window_%d" % b)
-            nc.vector.memset(window[b][:], 0.0)
+            if b < BLOCKS - 1:
+                nc.vector.memset(window[b][:], 0.0)
+            else:
+                nc.gpsimd.memset(window[b][:], 0.0)
 
         warm_in = keep.tile([P, 8], F32, name="warm_in")
         warm_out = keep.tile([P, 8], F32, name="warm_out")
-        nc.vector.memset(warm_in[:], 0.0)
+        nc.gpsimd.memset(warm_in[:], 0.0)
         nc.scalar.copy(out=warm_out[:], in_=warm_in[:])
 
         grouped = {}
@@ -96,36 +100,51 @@ def tile_routed_moe_kernel(tc, xT, w_words, w_scales, gate, offs, out):
             )
 
         for g in range(PASSES):
-            for t in range(PACK):
-                for lo, hi in CUTS:
-                    nc.vector.tensor_copy(out=grouped[g][:, lo:hi, t], in_=plane[g, t][:, 0:T].indirect(listed(lo, hi)))
+            for u in range(PACK // 2):
+                if (g, u) == DIRECT:
+                    for t in (2 * u, 2 * u + 1):
+                        for lo, hi in CUTS:
+                            nc.vector.tensor_copy(out=grouped[g][:, lo:hi, t], in_=plane[g, t][:, 0:T].indirect(listed(lo, hi)))
+                else:
+                    picked = keep.tile([P, 2, SLOTS], F32, name="picked_%d_%d" % (g, u))
+                    for i in range(2):
+                        for lo, hi in CUTS:
+                            nc.vector.tensor_copy(out=picked[:, i, lo:hi], in_=plane[g, 2 * u + i][:].indirect(listed(lo, hi)))
+                    for lo, hi in CUTS:
+                        nc.scalar.copy(out=grouped[g][:, lo:hi, 2 * u:2 * u + 2], in_=picked[:, :, lo:hi].rearrange("p i c -> p c i"))
         quantize(0, 0, 512)
         quantize(1, 0, 128)
         quantize(1, 128, 256)
         quantize(1, 256, 512)
 
-        for lo, hi in CUTS:
-            for b in range(BLOCKS):
-                feats = slice(b * P, (b + 1) * P)
-                acc = psum.tile([P, hi - lo], F32, name="acc_%d_%d" % (b, lo))
-                for e in range(lo // C, hi // C):
-                    for g in range(PASSES):
-                        nc.tensor.matmul_mx(
-                            out=acc[:, e * C - lo:(e + 1) * C - lo],
-                            lhsT=w_codes[e][:, g, feats].bitcast(FP8X4),
-                            lhsT_scale=w_plane[:, e * PASSES + g, feats],
-                            rhs=x_codes[g][:, e * C:(e + 1) * C].bitcast(FP8X4),
-                            rhs_scale=x_scales[g][:, e * C:(e + 1) * C],
-                            start=(g == 0),
-                            stop=(g == PASSES - 1),
-                        )
-                sums = keep.tile([P, hi - lo], F32, name="sums_%d_%d" % (b, lo))
-                nc.scalar.copy(out=sums[:], in_=acc[:])
-                nc.vector.tensor_tensor(
-                    out=window[b][:].indirect(listed(lo, hi)),
-                    in0=sums[:],
-                    in1=gate_sb[lo][:, b, :],
-                    op=MULT,
-                )
-                if hi == SLOTS:
-                    nc.sync.dma_start(out[feats, :], window[b][:])
+        def way_back(b, lo, hi):
+            feats = slice(b * P, (b + 1) * P)
+            acc = psum.tile([P, hi - lo], F32, name="acc_%d_%d" % (b, 0 if hi <= 2 * C else 1))
+            for e in range(lo // C, hi // C):
+                for g in range(PASSES):
+                    nc.tensor.matmul_mx(
+                        out=acc[:, e * C - lo:(e + 1) * C - lo],
+                        lhsT=w_codes[e][:, g, feats].bitcast(FP8X4),
+                        lhsT_scale=w_plane[:, e * PASSES + g, feats],
+                        rhs=x_codes[g][:, e * C:(e + 1) * C].bitcast(FP8X4),
+                        rhs_scale=x_scales[g][:, e * C:(e + 1) * C],
+                        start=(g == 0),
+                        stop=(g == PASSES - 1),
+                    )
+            sums = keep.tile([P, hi - lo], F32, name="sums_%d_%d" % (b, lo))
+            nc.scalar.copy(out=sums[:], in_=acc[:])
+            nc.vector.tensor_tensor(
+                out=window[b][:].indirect(listed(lo, hi)),
+                in0=sums[:],
+                in1=gate_first[:, b, :] if lo == 0 else gate_sb[b][:, lo - C:hi - C],
+                op=MULT,
+            )
+            if hi == SLOTS:
+                nc.sync.dma_start(out[feats, :], window[b][:])
+
+        for b in range(BLOCKS):
+            way_back(b, 0, 128)
+        way_back(0, 128, 256)
+        way_back(0, 256, 512)
+        for b in range(1, BLOCKS):
+            way_back(b, 128, 512)

@@ -16,14 +16,19 @@ MULT = mybir.AluOpType.mult
 
 P = 128
 PACK = 4
-K_PASS = P * PACK
-PASSES = K // K_PASS
+PASSES = K // (P * PACK)
 SLOTS = E * C
 BLOCKS = N // P
+PER_COLUMN = 16
+QUADRANT = 32
+SCALE_ROWS = 4
+WARM = 8
 
-CUTS = ((0, 128), (128, 512))
-PAD = 16
-DIRECT = (1, 1)
+GATHER_CUTS = ((0, C), (C, SLOTS))
+
+PAIR = 2
+PAIRS = PACK // PAIR
+LAST_PAIR = (PASSES - 1, PAIRS - 1)
 
 
 def tile_routed_moe_kernel(tc, xT, w_words, w_scales, gate, offs, out):
@@ -33,43 +38,48 @@ def tile_routed_moe_kernel(tc, xT, w_words, w_scales, gate, offs, out):
         keep = ctx.enter_context(tc.tile_pool(name="keep", bufs=1))
         psum = ctx.enter_context(tc.psum_pool(name="psum", bufs=1))
 
-        offsets = lists.tile([P, SLOTS // 16], U16, name="offsets")
+
+        offsets = lists.tile([P, SLOTS // PER_COLUMN], U16, name="offsets")
         nc.sync.dma_start(offsets[:], offs)
 
         def listed(lo, hi):
-            return offsets[:, lo // 16:hi // 16]
+            return offsets[:, lo // PER_COLUMN:hi // PER_COLUMN]
 
         planes_hbm = xT.rearrange("(g p t) n -> g p t n", p=P, t=PACK)
         plane = {}
         for g in range(PASSES):
-            for t in range(PACK):
-                width = T + PAD if (g, t // 2) == DIRECT else T
-                plane[g, t] = keep.tile([P, width], F32, name="plane_%d_%d" % (g, t))
-                nc.sync.dma_start(plane[g, t][:, 0:T], planes_hbm[g, :, t, :])
+            for u in range(PAIRS):
+                if (g, u) == LAST_PAIR:
+                    both = keep.tile([P, PAIR, T], F32, name="last_pair")
+                    views = [both[:, i, :] for i in range(PAIR)]
+                else:
+                    views = [keep.tile([P, T], F32, name="plane_%d_%d" % (g, PAIR * u + i))[:] for i in range(PAIR)]
+                for i in range(PAIR):
+                    plane[g, PAIR * u + i] = views[i]
+                    nc.sync.dma_start(views[i], planes_hbm[g, :, PAIR * u + i, :])
 
         w_plane = keep.tile([P, E * PASSES, N], U8, name="w_plane", align_bytes=64)
         nc.gpsimd.memset(w_plane[:].rearrange("p j n -> p (j n)").bitcast(F32), 0.0)
-        scales_hbm = w_scales.rearrange("e a (q r) n -> r q (e a) n", r=4)
-        for r in range(4):
-            nc.sync.dma_start(w_plane[r:P:32, :, :].bitcast(I32), scales_hbm[r].bitcast(I32))
+        scales_hbm = w_scales.rearrange("e g (q r) n -> r q (e g) n", r=SCALE_ROWS)
+        for r in range(SCALE_ROWS):
+            nc.sync.dma_start(w_plane[r:P:QUADRANT, :, :].bitcast(I32), scales_hbm[r].bitcast(I32))
 
         w_codes = {}
-        gate_sb = {}
-        gate_hbm = gate.rearrange("(b p) j -> p b j", p=P)
 
-        def load_weights(e):
+        def load_codes(e):
             w_codes[e] = keep.tile([P, PASSES, N], I32, name="w_codes_%d" % e, align_bytes=64)
-            nc.sync.dma_start(w_codes[e][:], w_words[e].rearrange("a p n r -> p a (n r)").bitcast(I32))
+            nc.sync.dma_start(w_codes[e][:], w_words[e].rearrange("g p n r -> p g (n r)").bitcast(I32))
 
-        load_weights(0)
+        load_codes(0)
         gate_first = keep.tile([P, BLOCKS, C], F32, name="gate_first")
-        nc.sync.dma_start(gate_first[:], gate_hbm[:, :, 0:C])
-        load_weights(1)
-        load_weights(2)
-        load_weights(3)
+        nc.sync.dma_start(gate_first[:], gate.rearrange("(b p) j -> p b j", p=P)[:, :, 0:C])
+        for e in range(1, E):
+            load_codes(e)
+        gate_rest = {}
         for b in range(BLOCKS):
-            gate_sb[b] = keep.tile([P, SLOTS - C], F32, name="gate_sb_%d" % b)
-            nc.sync.dma_start(gate_sb[b][:], gate[b * P:(b + 1) * P, C:SLOTS])
+            gate_rest[b] = keep.tile([P, SLOTS - C], F32, name="gate_rest_%d" % b)
+            nc.sync.dma_start(gate_rest[b][:], gate[b * P:(b + 1) * P, C:SLOTS])
+
 
         window = {}
         for b in range(BLOCKS):
@@ -79,10 +89,11 @@ def tile_routed_moe_kernel(tc, xT, w_words, w_scales, gate, offs, out):
             else:
                 nc.gpsimd.memset(window[b][:], 0.0)
 
-        warm_in = keep.tile([P, 8], F32, name="warm_in")
-        warm_out = keep.tile([P, 8], F32, name="warm_out")
+        warm_in = keep.tile([P, WARM], F32, name="warm_in")
+        warm_out = keep.tile([P, WARM], F32, name="warm_out")
         nc.gpsimd.memset(warm_in[:], 0.0)
         nc.scalar.copy(out=warm_out[:], in_=warm_in[:])
+
 
         grouped = {}
         x_codes = {}
@@ -92,32 +103,39 @@ def tile_routed_moe_kernel(tc, xT, w_words, w_scales, gate, offs, out):
             x_codes[g] = keep.tile([P, SLOTS], U32, name="x_codes_%d" % g, align_bytes=64)
             x_scales[g] = keep.tile([P, SLOTS], U8, name="x_scales_%d" % g, align_bytes=64)
 
+        def gather_pair(g, u):
+            if (g, u) == LAST_PAIR:
+                for t in range(PAIR * u, PAIR * (u + 1)):
+                    for lo, hi in GATHER_CUTS:
+                        nc.vector.tensor_copy(out=grouped[g][:, lo:hi, t], in_=plane[g, t].indirect(listed(lo, hi)))
+            else:
+                picked = keep.tile([P, PAIR, SLOTS], F32, name="picked_%d_%d" % (g, u))
+                for i in range(PAIR):
+                    for lo, hi in GATHER_CUTS:
+                        nc.vector.tensor_copy(out=picked[:, i, lo:hi], in_=plane[g, PAIR * u + i].indirect(listed(lo, hi)))
+                for lo, hi in GATHER_CUTS:
+                    nc.scalar.copy(
+                        out=grouped[g][:, lo:hi, PAIR * u:PAIR * (u + 1)],
+                        in_=picked[:, :, lo:hi].rearrange("p i j -> p j i"),
+                    )
+
         def quantize(g, lo, hi):
             nc.vector.quantize_mx(
                 out=x_codes[g][:, lo:hi].bitcast(FP8X4),
                 scales=x_scales[g][:, lo:hi],
-                in_=grouped[g][:, lo:hi, :].rearrange("p c t -> p (c t)"),
+                in_=grouped[g][:, lo:hi, :].rearrange("p j t -> p (j t)"),
             )
 
         for g in range(PASSES):
-            for u in range(PACK // 2):
-                if (g, u) == DIRECT:
-                    for t in (2 * u, 2 * u + 1):
-                        for lo, hi in CUTS:
-                            nc.vector.tensor_copy(out=grouped[g][:, lo:hi, t], in_=plane[g, t][:, 0:T].indirect(listed(lo, hi)))
-                else:
-                    picked = keep.tile([P, 2, SLOTS], F32, name="picked_%d_%d" % (g, u))
-                    for i in range(2):
-                        for lo, hi in CUTS:
-                            nc.vector.tensor_copy(out=picked[:, i, lo:hi], in_=plane[g, 2 * u + i][:].indirect(listed(lo, hi)))
-                    for lo, hi in CUTS:
-                        nc.scalar.copy(out=grouped[g][:, lo:hi, 2 * u:2 * u + 2], in_=picked[:, :, lo:hi].rearrange("p i c -> p c i"))
-        quantize(0, 0, 512)
-        quantize(1, 0, 128)
-        quantize(1, 128, 256)
-        quantize(1, 256, 512)
+            for u in range(PAIRS):
+                gather_pair(g, u)
+        for g in range(PASSES - 1):
+            quantize(g, 0, SLOTS)
+        for lo, hi in ((0, C), (C, 2 * C), (2 * C, SLOTS)):
+            quantize(PASSES - 1, lo, hi)
 
-        def way_back(b, lo, hi):
+
+        def sums_of(b, lo, hi):
             feats = slice(b * P, (b + 1) * P)
             acc = psum.tile([P, hi - lo], F32, name="acc_%d_%d" % (b, 0 if hi <= 2 * C else 1))
             for e in range(lo // C, hi // C):
@@ -133,18 +151,22 @@ def tile_routed_moe_kernel(tc, xT, w_words, w_scales, gate, offs, out):
                     )
             sums = keep.tile([P, hi - lo], F32, name="sums_%d_%d" % (b, lo))
             nc.scalar.copy(out=sums[:], in_=acc[:])
+            return sums
+
+        def way_back(b, lo, hi):
+            sums = sums_of(b, lo, hi)
             nc.vector.tensor_tensor(
                 out=window[b][:].indirect(listed(lo, hi)),
                 in0=sums[:],
-                in1=gate_first[:, b, :] if lo == 0 else gate_sb[b][:, lo - C:hi - C],
+                in1=gate_first[:, b, :] if lo == 0 else gate_rest[b][:, lo - C:hi - C],
                 op=MULT,
             )
             if hi == SLOTS:
-                nc.sync.dma_start(out[feats, :], window[b][:])
+                nc.sync.dma_start(out[b * P:(b + 1) * P, :], window[b][:])
 
         for b in range(BLOCKS):
-            way_back(b, 0, 128)
-        way_back(0, 128, 256)
-        way_back(0, 256, 512)
+            way_back(b, 0, C)
+        way_back(0, C, 2 * C)
+        way_back(0, 2 * C, SLOTS)
         for b in range(1, BLOCKS):
-            way_back(b, 128, 512)
+            way_back(b, C, SLOTS)

@@ -61,8 +61,13 @@ def tile_routed_moe_kernel(tc, xT, w_words, w_scales, gate, offs, out):
         w_plane = keep.tile([P, E * PASSES, N], U8, name="w_plane", align_bytes=64)
         nc.gpsimd.memset(w_plane[:].rearrange("p j n -> p (j n)").bitcast(F32), 0.0)
         scales_hbm = w_scales.rearrange("e g (q r) n -> r q (e g) n", r=SCALE_ROWS)
-        for r in range(SCALE_ROWS):
-            nc.sync.dma_start(w_plane[r:P:QUADRANT, :, :].bitcast(I32), scales_hbm[r].bitcast(I32))
+
+        def load_scales(first, last):
+            some = slice(first * PASSES, last * PASSES)
+            for r in range(SCALE_ROWS):
+                nc.sync.dma_start(w_plane[r:P:QUADRANT, some, :].bitcast(I32), scales_hbm[r][:, some, :].bitcast(I32))
+
+        load_scales(0, 1)
 
         w_codes = {}
 
@@ -73,6 +78,7 @@ def tile_routed_moe_kernel(tc, xT, w_words, w_scales, gate, offs, out):
         load_codes(0)
         gate_first = keep.tile([P, BLOCKS, C], F32, name="gate_first")
         nc.sync.dma_start(gate_first[:], gate.rearrange("(b p) j -> p b j", p=P)[:, :, 0:C])
+        load_scales(1, E)
         for e in range(1, E):
             load_codes(e)
         gate_rest = {}
@@ -103,21 +109,28 @@ def tile_routed_moe_kernel(tc, xT, w_words, w_scales, gate, offs, out):
             x_codes[g] = keep.tile([P, SLOTS], U32, name="x_codes_%d" % g, align_bytes=64)
             x_scales[g] = keep.tile([P, SLOTS], U8, name="x_scales_%d" % g, align_bytes=64)
 
+        four = {}
+
         def gather_pair(g, u):
             if (g, u) == LAST_PAIR:
                 for t in range(PAIR * u, PAIR * (u + 1)):
                     for lo, hi in GATHER_CUTS:
                         nc.vector.tensor_copy(out=grouped[g][:, lo:hi, t], in_=plane[g, t].indirect(listed(lo, hi)))
+            elif g < PASSES - 1:
+                if u == 0:
+                    four[g] = keep.tile([P, PACK, SLOTS], F32, name="four_%d" % g)
+                for t in range(PAIR * u, PAIR * (u + 1)):
+                    nc.vector.tensor_copy(out=four[g][:, t, :], in_=plane[g, t].indirect(offsets[:]))
+                if u == PAIRS - 1:
+                    nc.scalar.copy(out=grouped[g][:], in_=four[g][:].rearrange("p t j -> p j t"))
             else:
                 picked = keep.tile([P, PAIR, SLOTS], F32, name="picked_%d_%d" % (g, u))
                 for i in range(PAIR):
-                    for lo, hi in GATHER_CUTS:
-                        nc.vector.tensor_copy(out=picked[:, i, lo:hi], in_=plane[g, PAIR * u + i].indirect(listed(lo, hi)))
-                for lo, hi in GATHER_CUTS:
-                    nc.scalar.copy(
-                        out=grouped[g][:, lo:hi, PAIR * u:PAIR * (u + 1)],
-                        in_=picked[:, :, lo:hi].rearrange("p i j -> p j i"),
-                    )
+                    nc.vector.tensor_copy(out=picked[:, i, :], in_=plane[g, PAIR * u + i].indirect(offsets[:]))
+                nc.scalar.copy(
+                    out=grouped[g][:, :, PAIR * u:PAIR * (u + 1)],
+                    in_=picked[:].rearrange("p i j -> p j i"),
+                )
 
         def quantize(g, lo, hi):
             nc.vector.quantize_mx(

@@ -13,6 +13,7 @@ U16 = mybir.dt.uint16
 U8 = mybir.dt.uint8
 FP8X4 = mybir.dt.float8_e4m3fn_x4
 MULT = mybir.AluOpType.mult
+COPY = mybir.ActivationFunctionType.Copy
 
 P = 128
 PACK = 4
@@ -29,6 +30,7 @@ GATHER_CUTS = ((0, C), (C, SLOTS))
 PAIR = 2
 PAIRS = PACK // PAIR
 LAST_PAIR = (PASSES - 1, PAIRS - 1)
+HALF = SLOTS // 2
 
 
 def tile_routed_moe_kernel(tc, xT, w_words, w_scales, gate, offs, out):
@@ -113,9 +115,12 @@ def tile_routed_moe_kernel(tc, xT, w_words, w_scales, gate, offs, out):
 
         def gather_pair(g, u):
             if (g, u) == LAST_PAIR:
-                for t in range(PAIR * u, PAIR * (u + 1)):
-                    for lo, hi in GATHER_CUTS:
-                        nc.vector.tensor_copy(out=grouped[g][:, lo:hi, t], in_=plane[g, t].indirect(listed(lo, hi)))
+                rounded = keep.tile([P, PAIR, T], BF16, name="rounded")
+                for i in range(PAIR):
+                    t = PAIR * u + i
+                    nc.vector.tensor_copy(out=grouped[g][:, 0:HALF, t], in_=plane[g, t].indirect(listed(0, HALF)))
+                    nc.vector.tensor_copy(out=rounded[:, i, :], in_=plane[g, t])
+                    nc.scalar.activation(grouped[g][:, HALF:SLOTS, t], rounded[:, i, :].indirect(listed(HALF, SLOTS)), COPY)
             elif g < PASSES - 1:
                 if u == 0:
                     four[g] = keep.tile([P, PACK, SLOTS], F32, name="four_%d" % g)
@@ -144,7 +149,7 @@ def tile_routed_moe_kernel(tc, xT, w_words, w_scales, gate, offs, out):
                 gather_pair(g, u)
         for g in range(PASSES - 1):
             quantize(g, 0, SLOTS)
-        for lo, hi in ((0, C), (C, 2 * C), (2 * C, SLOTS)):
+        for lo, hi in ((0, HALF), (HALF, SLOTS)):
             quantize(PASSES - 1, lo, hi)
 
 

@@ -77,16 +77,23 @@ def tile_routed_moe_kernel(tc, xT, w_words, w_scales, gate, offs, out):
             w_codes[e] = keep.tile([P, PASSES, N], I32, name="w_codes_%d" % e, align_bytes=64)
             nc.sync.dma_start(w_codes[e][:], w_words[e].rearrange("g p n r -> p g (n r)").bitcast(I32))
 
+        gate_of = {}
+
+        def load_gate_columns(e):
+            gate_of[e] = keep.tile([P, BLOCKS, C], F32, name="gate_of_%d" % e)
+            nc.sync.dma_start(gate_of[e][:], gate.rearrange("(b p) j -> p b j", p=P)[:, :, e * C:(e + 1) * C])
+
         load_codes(0)
-        gate_first = keep.tile([P, BLOCKS, C], F32, name="gate_first")
-        nc.sync.dma_start(gate_first[:], gate.rearrange("(b p) j -> p b j", p=P)[:, :, 0:C])
+        load_gate_columns(0)
         load_scales(1, E)
-        for e in range(1, E):
+        load_codes(1)
+        load_gate_columns(1)
+        for e in range(2, E):
             load_codes(e)
         gate_rest = {}
         for b in range(BLOCKS):
-            gate_rest[b] = keep.tile([P, SLOTS - C], F32, name="gate_rest_%d" % b)
-            nc.sync.dma_start(gate_rest[b][:], gate[b * P:(b + 1) * P, C:SLOTS])
+            gate_rest[b] = keep.tile([P, SLOTS - HALF], F32, name="gate_rest_%d" % b)
+            nc.sync.dma_start(gate_rest[b][:], gate[b * P:(b + 1) * P, HALF:SLOTS])
 
 
         window = {}
@@ -176,15 +183,14 @@ def tile_routed_moe_kernel(tc, xT, w_words, w_scales, gate, offs, out):
             nc.vector.tensor_tensor(
                 out=window[b][:].indirect(listed(lo, hi)),
                 in0=sums[:],
-                in1=gate_first[:, b, :] if lo == 0 else gate_rest[b][:, lo - C:hi - C],
+                in1=gate_of[lo // C][:, b, :] if hi <= HALF else gate_rest[b][:],
                 op=MULT,
             )
             if hi == SLOTS:
                 nc.sync.dma_start(out[b * P:(b + 1) * P, :], window[b][:])
 
+        for e in range(2):
+            for b in range(BLOCKS):
+                way_back(b, e * C, (e + 1) * C)
         for b in range(BLOCKS):
-            way_back(b, 0, C)
-        way_back(0, C, 2 * C)
-        way_back(0, 2 * C, SLOTS)
-        for b in range(1, BLOCKS):
-            way_back(b, C, SLOTS)
+            way_back(b, HALF, SLOTS)

@@ -122,12 +122,11 @@ def tile_routed_moe_kernel(tc, xT, w_words, w_scales, gate, offs, out):
 
         def gather_pair(g, u):
             if (g, u) == LAST_PAIR:
-                rounded = keep.tile([P, PAIR, T], BF16, name="rounded")
-                for i in range(PAIR):
-                    t = PAIR * u + i
+                for t in range(PAIR * u, PAIR * (u + 1)):
+                    rounded = keep.tile([P, T], BF16, name="rounded_%d" % t)
                     nc.vector.tensor_copy(out=grouped[g][:, 0:HALF, t], in_=plane[g, t].indirect(listed(0, HALF)))
-                    nc.vector.tensor_copy(out=rounded[:, i, :], in_=plane[g, t])
-                    nc.scalar.activation(grouped[g][:, HALF:SLOTS, t], rounded[:, i, :].indirect(listed(HALF, SLOTS)), COPY)
+                    nc.gpsimd.tensor_copy(out=rounded[:], in_=plane[g, t])
+                    nc.scalar.activation(grouped[g][:, HALF:SLOTS, t], rounded[:].indirect(listed(HALF, SLOTS)), COPY)
             elif g < PASSES - 1:
                 if u == 0:
                     four[g] = keep.tile([P, PACK, SLOTS], F32, name="four_%d" % g)

@@ -30,6 +30,7 @@ GATHER_CUTS = ((0, C), (C, SLOTS))
 PAIR = 2
 PAIRS = PACK // PAIR
 LAST_PAIR = (PASSES - 1, PAIRS - 1)
+PIECE = 256
 HALF = SLOTS // 2
 
 
@@ -125,7 +126,8 @@ def tile_routed_moe_kernel(tc, xT, w_words, w_scales, gate, offs, out):
                 for t in range(PAIR * u, PAIR * (u + 1)):
                     rounded = keep.tile([P, T], BF16, name="rounded_%d" % t)
                     nc.vector.tensor_copy(out=grouped[g][:, 0:HALF, t], in_=plane[g, t].indirect(listed(0, HALF)))
-                    nc.gpsimd.tensor_copy(out=rounded[:], in_=plane[g, t])
+                    for c0 in range(0, T, PIECE):
+                        nc.gpsimd.tensor_copy(out=rounded[:, c0:c0 + PIECE], in_=plane[g, t][:, c0:c0 + PIECE])
                     nc.scalar.activation(grouped[g][:, HALF:SLOTS, t], rounded[:].indirect(listed(HALF, SLOTS)), COPY)
             elif g < PASSES - 1:
                 if u == 0:

@@ -30,7 +30,7 @@ GATHER_CUTS = ((0, C), (C, SLOTS))
 PAIR = 2
 PAIRS = PACK // PAIR
 LAST_PAIR = (PASSES - 1, PAIRS - 1)
-PIECE = 256
+PIECE = 512
 HALF = SLOTS // 2
 
 

@@ -31,6 +31,7 @@ PAIR = 2
 PAIRS = PACK // PAIR
 LAST_PAIR = (PASSES - 1, PAIRS - 1)
 PIECE = 512
+RUN = 4
 HALF = SLOTS // 2
 
 
@@ -135,14 +136,17 @@ def tile_routed_moe_kernel(tc, xT, w_words, w_scales, gate, offs, out):
                 for t in range(PAIR * u, PAIR * (u + 1)):
                     nc.vector.tensor_copy(out=four[g][:, t, :], in_=plane[g, t].indirect(offsets[:]))
                 if u == PAIRS - 1:
-                    nc.scalar.copy(out=grouped[g][:], in_=four[g][:].rearrange("p t j -> p j t"))
+                    nc.scalar.copy(
+                        out=grouped[g][:].rearrange("p (c i) t -> p c t i", i=RUN),
+                        in_=four[g][:].rearrange("p t (c i) -> p c t i", i=RUN),
+                    )
             else:
                 picked = keep.tile([P, PAIR, SLOTS], F32, name="picked_%d_%d" % (g, u))
                 for i in range(PAIR):
                     nc.vector.tensor_copy(out=picked[:, i, :], in_=plane[g, PAIR * u + i].indirect(offsets[:]))
                 nc.scalar.copy(
-                    out=grouped[g][:, :, PAIR * u:PAIR * (u + 1)],
-                    in_=picked[:].rearrange("p i j -> p j i"),
+                    out=grouped[g][:, :, PAIR * u:PAIR * (u + 1)].rearrange("p (c i) t -> p c t i", i=RUN),
+                    in_=picked[:].rearrange("p t (c i) -> p c t i", i=RUN),
                 )
 
         def quantize(g, lo, hi):

@@ -120,50 +120,21 @@ def tile_routed_moe_kernel(tc, xT, w_words, w_scales, gate, offs, out):
             x_codes[g] = keep.tile([P, SLOTS], U32, name="x_codes_%d" % g, align_bytes=64)
             x_scales[g] = keep.tile([P, SLOTS], U8, name="x_scales_%d" % g, align_bytes=64)
 
-        four = {}
+        LAST = PASSES - 1
 
-        def gather_pair(g, u):
-            if (g, u) == LAST_PAIR:
-                for t in range(PAIR * u, PAIR * (u + 1)):
-                    rounded = keep.tile([P, T], BF16, name="rounded_%d" % t)
-                    nc.vector.tensor_copy(out=grouped[g][:, 0:HALF, t], in_=plane[g, t].indirect(listed(0, HALF)))
-                    for c0 in range(0, T, PIECE):
-                        nc.gpsimd.tensor_copy(out=rounded[:, c0:c0 + PIECE], in_=plane[g, t][:, c0:c0 + PIECE])
-                    nc.scalar.activation(grouped[g][:, HALF:SLOTS, t], rounded[:].indirect(listed(HALF, SLOTS)), COPY)
-            elif g < PASSES - 1:
-                if u == 0:
-                    four[g] = keep.tile([P, PACK, SLOTS], F32, name="four_%d" % g)
-                for t in range(PAIR * u, PAIR * (u + 1)):
-                    nc.vector.tensor_copy(out=four[g][:, t, :], in_=plane[g, t].indirect(offsets[:]))
-                if u == PAIRS - 1:
-                    nc.scalar.copy(
-                        out=grouped[g][:].rearrange("p (c i) t -> p c t i", i=RUN),
-                        in_=four[g][:].rearrange("p t (c i) -> p c t i", i=RUN),
-                    )
-            else:
-                picked = keep.tile([P, PAIR, SLOTS], F32, name="picked_%d_%d" % (g, u))
-                for i in range(PAIR):
-                    nc.vector.tensor_copy(out=picked[:, i, :], in_=plane[g, PAIR * u + i].indirect(offsets[:]))
-                nc.scalar.copy(
-                    out=grouped[g][:, :, PAIR * u:PAIR * (u + 1)].rearrange("p (c i) t -> p c t i", i=RUN),
-                    in_=picked[:].rearrange("p t (c i) -> p c t i", i=RUN),
-                )
+        first_codes = keep.tile([P, C], U32, name="turn", align_bytes=64)
+
+        def codes_of(g, e):
+            if g == LAST and e == 0:
+                return first_codes[:]
+            return x_codes[g][:, e * C:(e + 1) * C]
 
         def quantize(g, lo, hi):
             nc.vector.quantize_mx(
-                out=x_codes[g][:, lo:hi].bitcast(FP8X4),
+                out=(first_codes[:] if (g, lo, hi) == (LAST, 0, C) else x_codes[g][:, lo:hi]).bitcast(FP8X4),
                 scales=x_scales[g][:, lo:hi],
                 in_=grouped[g][:, lo:hi, :].rearrange("p j t -> p (j t)"),
             )
-
-        for g in range(PASSES):
-            for u in range(PAIRS):
-                gather_pair(g, u)
-        for g in range(PASSES - 1):
-            quantize(g, 0, SLOTS)
-        for lo, hi in ((0, HALF), (HALF, SLOTS)):
-            quantize(PASSES - 1, lo, hi)
-
 
         def sums_of(b, lo, hi):
             feats = slice(b * P, (b + 1) * P)
@@ -174,7 +145,7 @@ def tile_routed_moe_kernel(tc, xT, w_words, w_scales, gate, offs, out):
                         out=acc[:, e * C - lo:(e + 1) * C - lo],
                         lhsT=w_codes[e][:, g, feats].bitcast(FP8X4),
                         lhsT_scale=w_plane[:, e * PASSES + g, feats],
-                        rhs=x_codes[g][:, e * C:(e + 1) * C].bitcast(FP8X4),
+                        rhs=codes_of(g, e).bitcast(FP8X4),
                         rhs_scale=x_scales[g][:, e * C:(e + 1) * C],
                         start=(g == 0),
                         stop=(g == PASSES - 1),
@@ -183,8 +154,7 @@ def tile_routed_moe_kernel(tc, xT, w_words, w_scales, gate, offs, out):
             nc.scalar.copy(out=sums[:], in_=acc[:])
             return sums
 
-        def way_back(b, lo, hi):
-            sums = sums_of(b, lo, hi)
+        def scatter(b, lo, hi, sums):
             nc.vector.tensor_tensor(
                 out=window[b][:].indirect(listed(lo, hi)),
                 in0=sums[:],
@@ -194,8 +164,38 @@ def tile_routed_moe_kernel(tc, xT, w_words, w_scales, gate, offs, out):
             if hi == SLOTS:
                 nc.sync.dma_start(out[b * P:(b + 1) * P, :], window[b][:])
 
-        for e in range(2):
-            for b in range(BLOCKS):
-                way_back(b, e * C, (e + 1) * C)
+        def interleave(dst, src):
+            nc.scalar.copy(
+                out=dst.rearrange("p (c i) t -> p c t i", i=RUN),
+                in_=src.rearrange("p t (c i) -> p c t i", i=RUN),
+            )
+
+        four = keep.tile([P, PACK, SLOTS], F32, name="four")
+        for t in range(PACK):
+            nc.vector.tensor_copy(out=four[:, t, :], in_=plane[0, t].indirect(offsets[:]))
+        interleave(grouped[0][:], four[:])
+        picked = keep.tile([P, PAIR, SLOTS], F32, name="picked")
+        for t in range(PAIR):
+            nc.vector.tensor_copy(out=picked[:, t, :], in_=plane[LAST, t].indirect(offsets[:]))
+        interleave(grouped[LAST][:, :, 0:PAIR], picked[:])
+        nc.vector.tensor_copy(out=grouped[LAST][:, 0:HALF, PAIR], in_=plane[LAST, PAIR].indirect(listed(0, HALF)))
+        rounded = keep.tile([P, T], BF16, name="rounded")
+        for c0 in range(0, T, PIECE):
+            nc.gpsimd.tensor_copy(out=rounded[:, c0:c0 + PIECE], in_=plane[LAST, PAIR][:, c0:c0 + PIECE])
+        nc.scalar.activation(grouped[LAST][:, HALF:SLOTS, PAIR], rounded[:].indirect(listed(HALF, SLOTS)), COPY)
+        nc.vector.tensor_copy(out=grouped[LAST][:, 0:HALF, PAIR + 1], in_=plane[LAST, PAIR + 1].indirect(listed(0, HALF)))
+        quantize(0, 0, SLOTS)
+        quantize(LAST, 0, C)
+        quantize(LAST, C, 2 * C)
         for b in range(BLOCKS):
-            way_back(b, HALF, SLOTS)
+            scatter(b, 0, C, sums_of(b, 0, C))
+
+        late = keep.tile([P, T], BF16, name="turn", align_bytes=64)
+        for c0 in range(0, T, PIECE):
+            nc.scalar.copy(out=late[:, c0:c0 + PIECE], in_=plane[LAST, PAIR + 1][:, c0:c0 + PIECE])
+        nc.scalar.activation(grouped[LAST][:, HALF:SLOTS, PAIR + 1], late[:].indirect(listed(HALF, SLOTS)), COPY)
+        quantize(LAST, HALF, SLOTS)
+        for b in range(BLOCKS):
+            scatter(b, C, 2 * C, sums_of(b, C, 2 * C))
+        for b in range(BLOCKS):
+            scatter(b, HALF, SLOTS, sums_of(b, HALF, SLOTS))

@@ -151,7 +151,10 @@ def tile_routed_moe_kernel(tc, xT, w_words, w_scales, gate, offs, out):
                         stop=(g == PASSES - 1),
                     )
             sums = keep.tile([P, hi - lo], F32, name="sums_%d_%d" % (b, lo))
-            nc.scalar.copy(out=sums[:], in_=acc[:])
+            if (b, lo) == (0, 0):
+                nc.vector.tensor_copy(out=sums[:], in_=acc[:])
+            else:
+                nc.scalar.copy(out=sums[:], in_=acc[:])
             return sums
 
         def scatter(b, lo, hi, sums):
@@ -183,7 +186,11 @@ def tile_routed_moe_kernel(tc, xT, w_words, w_scales, gate, offs, out):
         for c0 in range(0, T, PIECE):
             nc.gpsimd.tensor_copy(out=rounded[:, c0:c0 + PIECE], in_=plane[LAST, PAIR][:, c0:c0 + PIECE])
         nc.scalar.activation(grouped[LAST][:, HALF:SLOTS, PAIR], rounded[:].indirect(listed(HALF, SLOTS)), COPY)
-        nc.vector.tensor_copy(out=grouped[LAST][:, 0:HALF, PAIR + 1], in_=plane[LAST, PAIR + 1].indirect(listed(0, HALF)))
+        for e in range(2):
+            nc.vector.tensor_copy(
+                out=grouped[LAST][:, e * C:(e + 1) * C, PAIR + 1],
+                in_=plane[LAST, PAIR + 1].indirect(listed(e * C, (e + 1) * C)),
+            )
         quantize(0, 0, SLOTS)
         quantize(LAST, 0, C)
         quantize(LAST, C, 2 * C)

@@ -44,7 +44,6 @@ def tile_routed_moe_kernel(tc, xT, w_words, w_scales, gate, offs, out):
 
 
         offsets = lists.tile([P, SLOTS // PER_COLUMN], U16, name="offsets")
-        nc.sync.dma_start(offsets[:], offs)
 
         def listed(lo, hi):
             return offsets[:, lo // PER_COLUMN:hi // PER_COLUMN]
@@ -61,6 +60,8 @@ def tile_routed_moe_kernel(tc, xT, w_words, w_scales, gate, offs, out):
                 for i in range(PAIR):
                     plane[g, PAIR * u + i] = views[i]
                     nc.sync.dma_start(views[i], planes_hbm[g, :, PAIR * u + i, :])
+                    if (g, u, i) == (0, 0, 0):
+                        nc.sync.dma_start(offsets[:], offs)
 
         w_plane = keep.tile([P, E * PASSES, N], U8, name="w_plane", align_bytes=64)
         nc.gpsimd.memset(w_plane[:].rearrange("p j n -> p (j n)").bitcast(F32), 0.0)

@@ -102,10 +102,7 @@ def tile_routed_moe_kernel(tc, xT, w_words, w_scales, gate, offs, out):
         window = {}
         for b in range(BLOCKS):
             window[b] = keep.tile([P, T], F32, name="window_%d" % b)
-            if b < BLOCKS - 1:
-                nc.vector.memset(window[b][:], 0.0)
-            else:
-                nc.gpsimd.memset(window[b][:], 0.0)
+            nc.gpsimd.memset(window[b][:], 0.0)
 
         warm_in = keep.tile([P, WARM], F32, name="warm_in")
         warm_out = keep.tile([P, WARM], F32, name="warm_out")

from contextlib import ExitStack

import concourse.mybir as mybir

K, T, E, C, N = 1024, 1024, 4, 128, 512
FLOPS = 2 * K * N * E * C

F32 = mybir.dt.float32
BF16 = mybir.dt.bfloat16
I32 = mybir.dt.int32
U32 = mybir.dt.uint32
U16 = mybir.dt.uint16
U8 = mybir.dt.uint8
FP8X4 = mybir.dt.float8_e4m3fn_x4
MULT = mybir.AluOpType.mult
COPY = mybir.ActivationFunctionType.Copy

P = 128
PACK = 4
PASSES = K // (P * PACK)
SLOTS = E * C
BLOCKS = N // P
PER_COLUMN = 16
QUADRANT = 32
SCALE_ROWS = 4
WARM = 8

GATHER_CUTS = ((0, C), (C, SLOTS))

PAIR = 2
PAIRS = PACK // PAIR
LAST_PAIR = (PASSES - 1, PAIRS - 1)
PIECE = 512
RUN = 4
HALF = SLOTS // 2


def tile_routed_moe_kernel(tc, xT, w_words, w_scales, gate, offs, out):
    nc = tc.nc
    with ExitStack() as ctx:
        lists = ctx.enter_context(tc.tile_pool(name="lists", bufs=1))
        keep = ctx.enter_context(tc.tile_pool(name="keep", bufs=1))
        psum = ctx.enter_context(tc.psum_pool(name="psum", bufs=1))


        offsets = lists.tile([P, SLOTS // PER_COLUMN], U16, name="offsets")

        def listed(lo, hi):
            return offsets[:, lo // PER_COLUMN:hi // PER_COLUMN]

        planes_hbm = xT.rearrange("(g p t) n -> g p t n", p=P, t=PACK)
        plane = {}
        for g in range(PASSES):
            for u in range(PAIRS):
                if (g, u) == LAST_PAIR:
                    both = keep.tile([P, PAIR, T], F32, name="last_pair")
                    views = [both[:, i, :] for i in range(PAIR)]
                else:
                    views = [keep.tile([P, T], F32, name="plane_%d_%d" % (g, PAIR * u + i))[:] for i in range(PAIR)]
                for i in range(PAIR):
                    plane[g, PAIR * u + i] = views[i]
                    nc.sync.dma_start(views[i], planes_hbm[g, :, PAIR * u + i, :])
                    if (g, u, i) == (0, 0, 0):
                        nc.sync.dma_start(offsets[:], offs)

        w_plane = keep.tile([P, E * PASSES, N], U8, name="w_plane", align_bytes=64)
        nc.gpsimd.memset(w_plane[:].rearrange("p j n -> p (j n)").bitcast(F32), 0.0)
        scales_hbm = w_scales.rearrange("e g (q r) n -> r q (e g) n", r=SCALE_ROWS)

        def load_scales(first, last):
            some = slice(first * PASSES, last * PASSES)
            for r in range(SCALE_ROWS):
                nc.sync.dma_start(w_plane[r:P:QUADRANT, some, :].bitcast(I32), scales_hbm[r][:, some, :].bitcast(I32))

        load_scales(0, 1)

        w_codes = {}

        def load_codes(e):
            w_codes[e] = keep.tile([P, PASSES, N], I32, name="w_codes_%d" % e, align_bytes=64)
            nc.sync.dma_start(w_codes[e][:], w_words[e].rearrange("g p n r -> p g (n r)").bitcast(I32))

        gate_of = {}

        def load_gate_columns(e):
            gate_of[e] = keep.tile([P, BLOCKS, C], F32, name="gate_of_%d" % e)
            nc.sync.dma_start(gate_of[e][:], gate.rearrange("(b p) j -> p b j", p=P)[:, :, e * C:(e + 1) * C])

        load_codes(0)
        load_gate_columns(0)
        load_scales(1, E)
        load_codes(1)
        load_gate_columns(1)
        for e in range(2, E):
            load_codes(e)
        gate_rest = {}
        for b in range(BLOCKS):
            gate_rest[b] = keep.tile([P, SLOTS - HALF], F32, name="gate_rest_%d" % b)
            nc.sync.dma_start(gate_rest[b][:], gate[b * P:(b + 1) * P, HALF:SLOTS])


        window = {}
        for b in range(BLOCKS):
            window[b] = keep.tile([P, T], F32, name="window_%d" % b)
            nc.gpsimd.memset(window[b][:], 0.0)

        warm_in = keep.tile([P, WARM], F32, name="warm_in")
        warm_out = keep.tile([P, WARM], F32, name="warm_out")
        nc.gpsimd.memset(warm_in[:], 0.0)
        nc.scalar.copy(out=warm_out[:], in_=warm_in[:])


        grouped = {}
        x_codes = {}
        x_scales = {}
        for g in range(PASSES):
            grouped[g] = keep.tile([P, SLOTS, PACK], BF16, name="grouped_%d" % g, align_bytes=64)
            x_codes[g] = keep.tile([P, SLOTS], U32, name="x_codes_%d" % g, align_bytes=64)
            x_scales[g] = keep.tile([P, SLOTS], U8, name="x_scales_%d" % g, align_bytes=64)

        LAST = PASSES - 1

        first_codes = keep.tile([P, C], U32, name="turn", align_bytes=64)

        def codes_of(g, e):
            if g == LAST and e == 0:
                return first_codes[:]
            return x_codes[g][:, e * C:(e + 1) * C]

        def quantize(g, lo, hi):
            nc.vector.quantize_mx(
                out=(first_codes[:] if (g, lo, hi) == (LAST, 0, C) else x_codes[g][:, lo:hi]).bitcast(FP8X4),
                scales=x_scales[g][:, lo:hi],
                in_=grouped[g][:, lo:hi, :].rearrange("p j t -> p (j t)"),
            )

        def sums_of(b, lo, hi):
            feats = slice(b * P, (b + 1) * P)
            acc = psum.tile([P, hi - lo], F32, name="acc_%d_%d" % (b, 0 if hi <= 2 * C else 1))
            for e in range(lo // C, hi // C):
                for g in range(PASSES):
                    nc.tensor.matmul_mx(
                        out=acc[:, e * C - lo:(e + 1) * C - lo],
                        lhsT=w_codes[e][:, g, feats].bitcast(FP8X4),
                        lhsT_scale=w_plane[:, e * PASSES + g, feats],
                        rhs=codes_of(g, e).bitcast(FP8X4),
                        rhs_scale=x_scales[g][:, e * C:(e + 1) * C],
                        start=(g == 0),
                        stop=(g == PASSES - 1),
                    )
            sums = keep.tile([P, hi - lo], F32, name="sums_%d_%d" % (b, lo))
            if (b, lo) == (0, 0):
                nc.vector.tensor_copy(out=sums[:], in_=acc[:])
            else:
                nc.scalar.copy(out=sums[:], in_=acc[:])
            return sums

        def scatter(b, lo, hi, sums):
            nc.vector.tensor_tensor(
                out=window[b][:].indirect(listed(lo, hi)),
                in0=sums[:],
                in1=gate_of[lo // C][:, b, :] if hi <= HALF else gate_rest[b][:],
                op=MULT,
            )
            if hi == SLOTS:
                nc.sync.dma_start(out[b * P:(b + 1) * P, :], window[b][:])

        def interleave(dst, src):
            nc.scalar.copy(
                out=dst.rearrange("p (c i) t -> p c t i", i=RUN),
                in_=src.rearrange("p t (c i) -> p c t i", i=RUN),
            )

        four = keep.tile([P, PACK, SLOTS], F32, name="four")
        for t in range(PACK):
            nc.vector.tensor_copy(out=four[:, t, :], in_=plane[0, t].indirect(offsets[:]))
        interleave(grouped[0][:], four[:])
        picked = keep.tile([P, PAIR, SLOTS], F32, name="picked")
        for t in range(PAIR):
            nc.vector.tensor_copy(out=picked[:, t, :], in_=plane[LAST, t].indirect(offsets[:]))
        interleave(grouped[LAST][:, :, 0:PAIR], picked[:])
        nc.vector.tensor_copy(out=grouped[LAST][:, 0:HALF, PAIR], in_=plane[LAST, PAIR].indirect(listed(0, HALF)))
        rounded = keep.tile([P, T], BF16, name="rounded")
        for c0 in range(0, T, PIECE):
            nc.gpsimd.tensor_copy(out=rounded[:, c0:c0 + PIECE], in_=plane[LAST, PAIR][:, c0:c0 + PIECE])
        nc.scalar.activation(grouped[LAST][:, HALF:SLOTS, PAIR], rounded[:].indirect(listed(HALF, SLOTS)), COPY)
        for e in range(2):
            nc.vector.tensor_copy(
                out=grouped[LAST][:, e * C:(e + 1) * C, PAIR + 1],
                in_=plane[LAST, PAIR + 1].indirect(listed(e * C, (e + 1) * C)),
            )
        quantize(0, 0, SLOTS)
        quantize(LAST, 0, C)
        quantize(LAST, C, 2 * C)
        for b in range(BLOCKS):
            scatter(b, 0, C, sums_of(b, 0, C))

        late = keep.tile([P, T], BF16, name="turn", align_bytes=64)
        for c0 in range(0, T, PIECE):
            nc.scalar.copy(out=late[:, c0:c0 + PIECE], in_=plane[LAST, PAIR + 1][:, c0:c0 + PIECE])
        nc.scalar.activation(grouped[LAST][:, HALF:SLOTS, PAIR + 1], late[:].indirect(listed(HALF, SLOTS)), COPY)
        quantize(LAST, HALF, SLOTS)
        for b in range(BLOCKS):
            scatter(b, C, 2 * C, sums_of(b, C, 2 * C))
        for b in range(BLOCKS):
            scatter(b, HALF, SLOTS, sums_of(b, HALF, SLOTS))
